import numpy as np, ml_dtypes
CORES = [24,48,72,152,176,200]
N = 6
KT, C = 4, 64
B = 2
def setup_inputs(rng):
    return {"x": rng.standard_normal((N, 128, KT * C), dtype=np.float32).astype(ml_dtypes.bfloat16)}
def setup_inputs_big(rng):
    d = setup_inputs(rng)
    for k in ("x",): d[k] = (d[k].astype(np.float32) * 1024.0).astype(d[k].dtype)
    return d
def setup_inputs_small(rng):
    d = setup_inputs(rng)
    for k in ("x",): d[k] = (d[k].astype(np.float32) * (1 / 1024.0)).astype(d[k].dtype)
    return d
def setup_inputs_apart(rng):
    d = setup_inputs(rng)
    f = (10.0 ** rng.permutation(np.linspace(-1.5, 1.5, N))).astype(np.float32).reshape(N, 1, 1)
    for k in ("x",): d[k] = (d[k].astype(np.float32) * f).astype(d[k].dtype)
    return d
def reference(x):
    X = x.astype(np.float64)
    y = np.full((N, C, (2 * B + 1) * C), np.nan)
    for r in range(N):
        for i in range(2 * B + 1):
            s = (r + i - B) % N
            if s != r: y[r][:, C * i:C * i + C] = sum(X[r][:, C * t:C * t + C].T @ X[s][:, C * t:C * t + C] for t in range(KT))
    return {"y": y.astype(ml_dtypes.bfloat16 if x.dtype != np.float64 else np.float64)}

@@ -1,0 +1,146 @@
+from concourse.bass import DstId, RemoteDMATransfer
+
+NSIM = 256
+KT, C, B = 4, 64, 2
+W = KT * C
+BLOCKS = [i for i in range(2 * B + 1) if i != B]
+
+SCRATCH = {
+    "xd": ("dram", [128, W], "bfloat16"),
+    "xs": ("sbuf", [128, W], "bfloat16"),
+    "land": ("sbuf", [128, len(BLOCKS) * W], "bfloat16"),
+    "yb": ("sbuf", [C, len(BLOCKS) * C], "bfloat16"),
+    "ps0": ("psum", [128, 512], "float32"),
+    "ps1": ("psum", [128, 512], "float32"),
+    "ps2": ("psum", [128, 512], "float32"),
+    "ps3": ("psum", [128, 512], "float32"),
+}
+SEMAPHORES = ["ldd", "lds", "rel", "sent", "arr0", "arr1", "arr2", "arr3", "mm0", "mm1", "mm2", "mm3", "cpl", "cpr", "st"]
+
+
+def _bits(m):
+    return [b for b in range(m.bit_length()) if (m >> b) & 1]
+
+
+def _mask(bits):
+    m = 0
+    for b in bits:
+        m |= 1 << b
+    return m
+
+
+def _count(m):
+    return len(_bits(m))
+
+
+def _deal(engines, k):
+    if k == 0:
+        return []
+    per = 1
+    while 2 * per <= len(engines) // k:
+        per *= 2
+    return [_mask(engines[j::k][:per]) for j in range(k)]
+
+
+def _routes(T, topo):
+    cores = list(T.cores)
+    n = len(cores)
+    planes = []
+    for r in range(n):
+        home = [q for q in planes if topo.same_plane(cores[q[0]], cores[r])]
+        if home:
+            home[0].append(r)
+        else:
+            planes.append([r])
+    pos = {}
+    for q in planes:
+        for k, r in enumerate(q):
+            pos[r] = k
+    routes = []
+    for s in range(n):
+        src = cores[s]
+        chipmates = [c for c in range(NSIM) if c != src and T.rank_of(c) is None
+                     and topo.host(c) == topo.host(src) and topo.chip(c) == topo.chip(src)]
+        mine, used = [], []
+        for slot, i in enumerate(BLOCKS):
+            r = (s - i + B) % n
+            relay = None
+            if not topo.may_write(src, cores[r]):
+                owners = [c for c in chipmates if topo.may_write(c, cores[r])]
+                dies = sorted(set(topo.die(c) for c in owners))
+                want = dies[(pos[s] + pos[r]) % len(dies)]
+                relay = [c for c in owners if topo.die(c) == want and c not in used][0]
+                used.append(relay)
+            mine.append({"src": s, "dst": r, "slot": slot, "relay": relay})
+        direct = [m for m in mine if m["relay"] is None]
+        hop = [m for m in mine if m["relay"] is not None]
+        off = _bits(topo.mask(src, cores[direct[0]["dst"]])) if direct else []
+        on = _bits(topo.mask(src, hop[0]["relay"])) if hop else []
+        for m, k in zip(hop, _deal([b for b in on if b not in off], len(hop))):
+            m["m1"], m["m2"] = k, topo.mask(m["relay"], cores[m["dst"]])
+        for m, k in zip(direct, _deal(off, len(direct))):
+            m["m1"], m["m2"] = k, 0
+        routes += mine
+    return routes
+
+
+def _slot(T, j):
+    return T.land[:, j * W:(j + 1) * W]
+
+
+def rank_program(g, core, T, topo):
+    sem = T.sem
+    cores = list(T.cores)
+    routes = _routes(T, topo)
+
+    for m in routes:
+        if m["relay"] == core:
+            rid, pid = topo.addr(cores[m["dst"]], core)
+            g.wait_ge(sem.rel, _count(m["m1"]))
+            g.remote_dma(out_ap=_slot(T, m["slot"]), in_ap=T.xd[:], remote_sem=sem["arr%d" % m["slot"]], local_sem=sem.sent,
+                         pid=pid, routing_id=rid, dma_engine_mask=m["m2"])
+            g.wait_ge(sem.sent, _count(m["m2"]))
+            return
+
+    rank = T.rank_of(core)
+    if rank is None:
+        return
+
+    g.sync.dma_start(T.xd[:], T.x[:]).then_inc(sem.ldd, 16)
+    g.sync.dma_start(T.xs[:], T.x[:]).then_inc(sem.lds, 16)
+    mine = [m for m in routes if m["src"] == rank]
+    g.wait_ge(sem.ldd, 16)
+    sent = 0
+    for batch in ([m for m in mine if m["relay"] is not None], [m for m in mine if m["relay"] is None]):
+        trs = []
+        for m in batch:
+            if m["relay"] is not None:
+                to, out, rsem = m["relay"], T.xd[:], sem.rel
+            else:
+                to, out, rsem = cores[m["dst"]], _slot(T, m["slot"]), sem["arr%d" % m["slot"]]
+            rid, pid = topo.addr(to, core)
+            trs.append(RemoteDMATransfer(dst_ids=[DstId(rid=rid, pnc=pid)], dma_engine_mask=m["m1"], remote_sem=rsem,
+                                         src=T.xd[:], dst=out))
+            sent += _count(m["m1"])
+        if trs:
+            g.remote_dma_fused(trs, local_sem=sem.sent)
+
+    inbound = sorted([m for m in routes if m["dst"] == rank], key=lambda m: (m["relay"] is not None, m["slot"]))
+    g.tensor.wait_ge(sem.lds, 16)
+    for m in inbound:
+        j = m["slot"]
+        ps = T["ps%d" % j][0:C, 0:C]
+        g.tensor.wait_ge(sem["arr%d" % j], _count(m["m2"] if m["relay"] is not None else m["m1"]))
+        for t in range(KT):
+            mm = g.tensor.matmul(ps, T.xs[:, t * C:(t + 1) * C], T.land[:, j * W + t * C:j * W + (t + 1) * C],
+                                 t == 0, t == KT - 1)
+        mm.then_inc(sem["mm%d" % j], 1)
+        g.vector.wait_ge(sem["mm%d" % j], 1)
+        g.vector.tensor_copy(T.yb[:, j * C:(j + 1) * C], ps).then_inc(sem.cpl if j < B else sem.cpr, 1)
+
+    g.sync.wait_ge(sem.cpl, B)
+    g.sync.dma_start(T.y[:, 0:B * C], T.yb[:, 0:B * C]).then_inc(sem.st, 16)
+    g.scalar.wait_ge(sem.cpr, B)
+    g.scalar.dma_start(T.y[:, (B + 1) * C:(2 * B + 1) * C], T.yb[:, B * C:2 * B * C]).then_inc(sem.st, 16)
+    g.wait_ge(sem.sent, sent)
+    g.wait_ge(sem.st, 32)

@@ -3,11 +3,17 @@ from concourse.bass import DstId, RemoteDMATransfer
 NSIM = 256
 KT, C, B = 4, 64, 2
 W = KT * C
+CA = C
+CB = W - CA
+RA = 128 * CA // W
 BLOCKS = [i for i in range(2 * B + 1) if i != B]
 
 SCRATCH = {
-    "xd": ("dram", [128, W], "bfloat16"),
-    "xs": ("sbuf", [128, W], "bfloat16"),
+    "xdA": ("dram", [128, CA], "bfloat16"),
+    "xdB": ("dram", [128, CB], "bfloat16"),
+    "xsA": ("sbuf", [128, CA], "bfloat16"),
+    "xsB": ("sbuf", [128, CB], "bfloat16"),
+    "xsN": ("sbuf", [128, W], "bfloat16"),
     "land": ("sbuf", [128, len(BLOCKS) * W], "bfloat16"),
     "yb": ("sbuf", [C, len(BLOCKS) * C], "bfloat16"),
     "ps0": ("psum", [128, 512], "float32"),
@@ -15,7 +21,9 @@ SCRATCH = {
     "ps2": ("psum", [128, 512], "float32"),
     "ps3": ("psum", [128, 512], "float32"),
 }
-SEMAPHORES = ["ldd", "lds", "rel", "sent", "arr0", "arr1", "arr2", "arr3", "mm0", "mm1", "mm2", "mm3", "cpl", "cpr", "st"]
+SEMAPHORES = ["ldA", "ldB", "lsA", "lsB", "lsN", "relA", "relB", "sent",
+              "arr0", "arr1", "arr2", "arr3", "arb0", "arb1", "arb2", "arb3",
+              "mm0", "mm1", "mm2", "mm3", "cpl", "cpr", "st"]
 
 
 def _bits(m):
@@ -84,10 +92,6 @@ def _routes(T, topo):
     return routes
 
 
-def _slot(T, j):
-    return T.land[:, j * W:(j + 1) * W]
-
-
 def rank_program(g, core, T, topo):
     sem = T.sem
     cores = list(T.cores)
@@ -96,47 +100,87 @@ def rank_program(g, core, T, topo):
     for m in routes:
         if m["relay"] == core:
             rid, pid = topo.addr(cores[m["dst"]], core)
-            g.wait_ge(sem.rel, _count(m["m1"]))
-            g.remote_dma(out_ap=_slot(T, m["slot"]), in_ap=T.xd[:], remote_sem=sem["arr%d" % m["slot"]], local_sem=sem.sent,
+            j = m["slot"]
+            g.wait_ge(sem.relA, _count(m["m1"]))
+            g.remote_dma(out_ap=T.land[:, j * W:j * W + CA], in_ap=T.xdA[:], remote_sem=sem["arr%d" % j], local_sem=sem.sent,
                          pid=pid, routing_id=rid, dma_engine_mask=m["m2"])
-            g.wait_ge(sem.sent, _count(m["m2"]))
+            g.wait_ge(sem.relB, _count(m["m1"]))
+            g.remote_dma(out_ap=T.land[:, j * W + CA:(j + 1) * W], in_ap=T.xdB[:], remote_sem=sem["arb%d" % j],
+                         local_sem=sem.sent, pid=pid, routing_id=rid, dma_engine_mask=m["m2"])
+            g.wait_ge(sem.sent, 2 * _count(m["m2"]))
             return
 
     rank = T.rank_of(core)
     if rank is None:
         return
 
-    g.sync.dma_start(T.xd[:], T.x[:]).then_inc(sem.ldd, 16)
-    g.sync.dma_start(T.xs[:], T.x[:]).then_inc(sem.lds, 16)
     mine = [m for m in routes if m["src"] == rank]
-    g.wait_ge(sem.ldd, 16)
-    sent = 0
-    for batch in ([m for m in mine if m["relay"] is not None], [m for m in mine if m["relay"] is None]):
-        trs = []
-        for m in batch:
-            if m["relay"] is not None:
-                to, out, rsem = m["relay"], T.xd[:], sem.rel
-            else:
-                to, out, rsem = cores[m["dst"]], _slot(T, m["slot"]), sem["arr%d" % m["slot"]]
-            rid, pid = topo.addr(to, core)
-            trs.append(RemoteDMATransfer(dst_ids=[DstId(rid=rid, pnc=pid)], dma_engine_mask=m["m1"], remote_sem=rsem,
-                                         src=T.xd[:], dst=out))
-            sent += _count(m["m1"])
-        if trs:
-            g.remote_dma_fused(trs, local_sem=sem.sent)
+    hop = [m for m in mine if m["relay"] is not None]
+    direct = [m for m in mine if m["relay"] is None]
 
-    inbound = sorted([m for m in routes if m["dst"] == rank], key=lambda m: (m["relay"] is not None, m["slot"]))
-    g.tensor.wait_ge(sem.lds, 16)
-    for m in inbound:
-        j = m["slot"]
-        ps = T["ps%d" % j][0:C, 0:C]
-        g.tensor.wait_ge(sem["arr%d" % j], _count(m["m2"] if m["relay"] is not None else m["m1"]))
-        for t in range(KT):
-            mm = g.tensor.matmul(ps, T.xs[:, t * C:(t + 1) * C], T.land[:, j * W + t * C:j * W + (t + 1) * C],
-                                 t == 0, t == KT - 1)
+    g.sync.dma_start(T.xdA[:], T.x[0:RA, :]).then_inc(sem.ldA, 16)
+    g.scalar.dma_start(T.xdB[:], T.x[RA:128, :]).then_inc(sem.ldB, 16)
+    if direct:
+        g.sync.dma_start(T.xsN[:], T.x[:]).then_inc(sem.lsN, 16)
+    g.sync.wait_ge(sem.ldA, 16)
+    g.sync.dma_start(T.xsA[:], T.xdA[:]).then_inc(sem.lsA, 16)
+    g.scalar.wait_ge(sem.ldB, 16)
+    g.scalar.dma_start(T.xsB[:], T.xdB[:]).then_inc(sem.lsB, 16)
+
+    sent = 0
+    for ld, buf, rsem in ((sem.ldA, T.xdA, sem.relA), (sem.ldB, T.xdB, sem.relB)):
+        g.wait_ge(ld, 16)
+        trs = []
+        for m in hop:
+            rid, pid = topo.addr(m["relay"], core)
+            trs.append(RemoteDMATransfer(dst_ids=[DstId(rid=rid, pnc=pid)], dma_engine_mask=m["m1"], remote_sem=rsem,
+                                         src=buf[:], dst=buf[:]))
+            sent += _count(m["m1"])
+        g.remote_dma_fused(trs, local_sem=sem.sent)
+    if direct:
+        g.wait_ge(sem.lsN, 16)
+        trs = []
+        for m in direct:
+            j = m["slot"]
+            rid, pid = topo.addr(cores[m["dst"]], core)
+            trs.append(RemoteDMATransfer(dst_ids=[DstId(rid=rid, pnc=pid)], dma_engine_mask=m["m1"],
+                                         remote_sem=sem["arr%d" % j], src=T.xsN[:], dst=T.land[:, j * W:(j + 1) * W]))
+            sent += _count(m["m1"])
+        g.remote_dma_fused(trs, local_sem=sem.sent)
+
+    inbound = sorted([m for m in routes if m["dst"] == rank], key=lambda m: m["slot"])
+
+    def done(mm, j):
         mm.then_inc(sem["mm%d" % j], 1)
         g.vector.wait_ge(sem["mm%d" % j], 1)
-        g.vector.tensor_copy(T.yb[:, j * C:(j + 1) * C], ps).then_inc(sem.cpl if j < B else sem.cpr, 1)
+        g.vector.tensor_copy(T.yb[:, j * C:(j + 1) * C], T["ps%d" % j][0:C, 0:C]).then_inc(sem.cpl if j < B else sem.cpr, 1)
+
+    if direct:
+        g.tensor.wait_ge(sem.lsN, 16)
+    for m in inbound:
+        if m["relay"] is None:
+            j = m["slot"]
+            g.tensor.wait_ge(sem["arr%d" % j], _count(m["m1"]))
+            for t in range(KT):
+                mm = g.tensor.matmul(T["ps%d" % j][0:C, 0:C], T.xsN[:, t * C:(t + 1) * C],
+                                     T.land[:, j * W + t * C:j * W + (t + 1) * C], t == 0, t == KT - 1)
+            done(mm, j)
+    g.tensor.wait_ge(sem.lsA, 16)
+    for m in inbound:
+        if m["relay"] is not None:
+            j = m["slot"]
+            g.tensor.wait_ge(sem["arr%d" % j], _count(m["m2"]))
+            g.tensor.matmul(T["ps%d" % j][0:C, 0:C], T.xsA[:, 0:C], T.land[:, j * W:j * W + C], True, False)
+    g.tensor.wait_ge(sem.lsB, 16)
+    nb = CB // C
+    for m in inbound:
+        if m["relay"] is not None:
+            j = m["slot"]
+            g.tensor.wait_ge(sem["arb%d" % j], _count(m["m2"]))
+            for k in range(nb):
+                mm = g.tensor.matmul(T["ps%d" % j][0:C, 0:C], T.xsB[:, k * C:(k + 1) * C],
+                                     T.land[:, j * W + CA + k * C:j * W + CA + (k + 1) * C], False, k == nb - 1)
+            done(mm, j)
 
     g.sync.wait_ge(sem.cpl, B)
     g.sync.dma_start(T.y[:, 0:B * C], T.yb[:, 0:B * C]).then_inc(sem.st, 16)

from concourse.bass import DstId, RemoteDMATransfer

NSIM = 256
KT, C, B = 4, 64, 2
W = KT * C
CA = C
CB = W - CA
RA = 128 * CA // W
BLOCKS = [i for i in range(2 * B + 1) if i != B]

SCRATCH = {
    "xdA": ("dram", [128, CA], "bfloat16"),
    "xdB": ("dram", [128, CB], "bfloat16"),
    "xsA": ("sbuf", [128, CA], "bfloat16"),
    "xsB": ("sbuf", [128, CB], "bfloat16"),
    "xsN": ("sbuf", [128, W], "bfloat16"),
    "land": ("sbuf", [128, len(BLOCKS) * W], "bfloat16"),
    "yb": ("sbuf", [C, len(BLOCKS) * C], "bfloat16"),
    "ps0": ("psum", [128, 512], "float32"),
    "ps1": ("psum", [128, 512], "float32"),
    "ps2": ("psum", [128, 512], "float32"),
    "ps3": ("psum", [128, 512], "float32"),
}
SEMAPHORES = ["ldA", "ldB", "lsA", "lsB", "lsN", "relA", "relB", "sent",
              "arr0", "arr1", "arr2", "arr3", "arb0", "arb1", "arb2", "arb3",
              "mm0", "mm1", "mm2", "mm3", "cpl", "cpr", "st"]


def _bits(m):
    return [b for b in range(m.bit_length()) if (m >> b) & 1]


def _mask(bits):
    m = 0
    for b in bits:
        m |= 1 << b
    return m


def _count(m):
    return len(_bits(m))


def _deal(engines, k):
    if k == 0:
        return []
    per = 1
    while 2 * per <= len(engines) // k:
        per *= 2
    return [_mask(engines[j::k][:per]) for j in range(k)]


def _routes(T, topo):
    cores = list(T.cores)
    n = len(cores)
    planes = []
    for r in range(n):
        home = [q for q in planes if topo.same_plane(cores[q[0]], cores[r])]
        if home:
            home[0].append(r)
        else:
            planes.append([r])
    pos = {}
    for q in planes:
        for k, r in enumerate(q):
            pos[r] = k
    routes = []
    for s in range(n):
        src = cores[s]
        chipmates = [c for c in range(NSIM) if c != src and T.rank_of(c) is None
                     and topo.host(c) == topo.host(src) and topo.chip(c) == topo.chip(src)]
        mine, used = [], []
        for slot, i in enumerate(BLOCKS):
            r = (s - i + B) % n
            relay = None
            if not topo.may_write(src, cores[r]):
                owners = [c for c in chipmates if topo.may_write(c, cores[r])]
                dies = sorted(set(topo.die(c) for c in owners))
                want = dies[(pos[s] + pos[r]) % len(dies)]
                relay = [c for c in owners if topo.die(c) == want and c not in used][0]
                used.append(relay)
            mine.append({"src": s, "dst": r, "slot": slot, "relay": relay})
        direct = [m for m in mine if m["relay"] is None]
        hop = [m for m in mine if m["relay"] is not None]
        off = _bits(topo.mask(src, cores[direct[0]["dst"]])) if direct else []
        on = _bits(topo.mask(src, hop[0]["relay"])) if hop else []
        for m, k in zip(hop, _deal([b for b in on if b not in off], len(hop))):
            m["m1"], m["m2"] = k, topo.mask(m["relay"], cores[m["dst"]])
        for m, k in zip(direct, _deal(off, len(direct))):
            m["m1"], m["m2"] = k, 0
        routes += mine
    return routes


def rank_program(g, core, T, topo):
    sem = T.sem
    cores = list(T.cores)
    routes = _routes(T, topo)

    for m in routes:
        if m["relay"] == core:
            rid, pid = topo.addr(cores[m["dst"]], core)
            j = m["slot"]
            g.wait_ge(sem.relA, _count(m["m1"]))
            g.remote_dma(out_ap=T.land[:, j * W:j * W + CA], in_ap=T.xdA[:], remote_sem=sem["arr%d" % j], local_sem=sem.sent,
                         pid=pid, routing_id=rid, dma_engine_mask=m["m2"])
            g.wait_ge(sem.relB, _count(m["m1"]))
            g.remote_dma(out_ap=T.land[:, j * W + CA:(j + 1) * W], in_ap=T.xdB[:], remote_sem=sem["arb%d" % j],
                         local_sem=sem.sent, pid=pid, routing_id=rid, dma_engine_mask=m["m2"])
            g.wait_ge(sem.sent, 2 * _count(m["m2"]))
            return

    rank = T.rank_of(core)
    if rank is None:
        return

    mine = [m for m in routes if m["src"] == rank]
    hop = [m for m in mine if m["relay"] is not None]
    direct = [m for m in mine if m["relay"] is None]

    g.sync.dma_start(T.xdA[:], T.x[0:RA, :]).then_inc(sem.ldA, 16)
    g.scalar.dma_start(T.xdB[:], T.x[RA:128, :]).then_inc(sem.ldB, 16)
    if direct:
        g.sync.dma_start(T.xsN[:], T.x[:]).then_inc(sem.lsN, 16)
    g.sync.wait_ge(sem.ldA, 16)
    g.sync.dma_start(T.xsA[:], T.xdA[:]).then_inc(sem.lsA, 16)
    g.scalar.wait_ge(sem.ldB, 16)
    g.scalar.dma_start(T.xsB[:], T.xdB[:]).then_inc(sem.lsB, 16)

    sent = 0
    for ld, buf, rsem in ((sem.ldA, T.xdA, sem.relA), (sem.ldB, T.xdB, sem.relB)):
        g.wait_ge(ld, 16)
        trs = []
        for m in hop:
            rid, pid = topo.addr(m["relay"], core)
            trs.append(RemoteDMATransfer(dst_ids=[DstId(rid=rid, pnc=pid)], dma_engine_mask=m["m1"], remote_sem=rsem,
                                         src=buf[:], dst=buf[:]))
            sent += _count(m["m1"])
        g.remote_dma_fused(trs, local_sem=sem.sent)
    if direct:
        g.wait_ge(sem.lsN, 16)
        trs = []
        for m in direct:
            j = m["slot"]
            rid, pid = topo.addr(cores[m["dst"]], core)
            trs.append(RemoteDMATransfer(dst_ids=[DstId(rid=rid, pnc=pid)], dma_engine_mask=m["m1"],
                                         remote_sem=sem["arr%d" % j], src=T.xsN[:], dst=T.land[:, j * W:(j + 1) * W]))
            sent += _count(m["m1"])
        g.remote_dma_fused(trs, local_sem=sem.sent)

    inbound = sorted([m for m in routes if m["dst"] == rank], key=lambda m: m["slot"])

    def done(mm, j):
        mm.then_inc(sem["mm%d" % j], 1)
        g.vector.wait_ge(sem["mm%d" % j], 1)
        g.vector.tensor_copy(T.yb[:, j * C:(j + 1) * C], T["ps%d" % j][0:C, 0:C]).then_inc(sem.cpl if j < B else sem.cpr, 1)

    if direct:
        g.tensor.wait_ge(sem.lsN, 16)
    for m in inbound:
        if m["relay"] is None:
            j = m["slot"]
            g.tensor.wait_ge(sem["arr%d" % j], _count(m["m1"]))
            for t in range(KT):
                mm = g.tensor.matmul(T["ps%d" % j][0:C, 0:C], T.xsN[:, t * C:(t + 1) * C],
                                     T.land[:, j * W + t * C:j * W + (t + 1) * C], t == 0, t == KT - 1)
            done(mm, j)
    g.tensor.wait_ge(sem.lsA, 16)
    for m in inbound:
        if m["relay"] is not None:
            j = m["slot"]
            g.tensor.wait_ge(sem["arr%d" % j], _count(m["m2"]))
            g.tensor.matmul(T["ps%d" % j][0:C, 0:C], T.xsA[:, 0:C], T.land[:, j * W:j * W + C], True, False)
    g.tensor.wait_ge(sem.lsB, 16)
    nb = CB // C
    for m in inbound:
        if m["relay"] is not None:
            j = m["slot"]
            g.tensor.wait_ge(sem["arb%d" % j], _count(m["m2"]))
            for k in range(nb):
                mm = g.tensor.matmul(T["ps%d" % j][0:C, 0:C], T.xsB[:, k * C:(k + 1) * C],
                                     T.land[:, j * W + CA + k * C:j * W + CA + (k + 1) * C], False, k == nb - 1)
            done(mm, j)

    g.sync.wait_ge(sem.cpl, B)
    g.sync.dma_start(T.y[:, 0:B * C], T.yb[:, 0:B * C]).then_inc(sem.st, 16)
    g.scalar.wait_ge(sem.cpr, B)
    g.scalar.dma_start(T.y[:, (B + 1) * C:(2 * B + 1) * C], T.yb[:, B * C:2 * B * C]).then_inc(sem.st, 16)
    g.wait_ge(sem.sent, sent)
    g.wait_ge(sem.st, 32)
